import numpy as np
import ml_dtypes


def mxq(x, axis, fmt="e4m3"):
    dtype, down = {"e4m3": (ml_dtypes.float8_e4m3fn, 7), "e5m2": (ml_dtypes.float8_e5m2, 14)}[fmt]
    v = np.moveaxis(np.asarray(x, np.float32).astype(ml_dtypes.bfloat16).astype(np.float64), axis, -1)
    blocks = v.reshape(v.shape[:-1] + (-1, 32))
    amax = np.abs(blocks).max(-1, keepdims=True)
    byte = np.maximum(np.where(amax > 0, np.frexp(amax)[1] - 1 + 127, 0) - down, 1)
    scale = np.exp2(byte - 127.0)
    codes = (blocks / scale).astype(np.float32).astype(dtype).astype(np.float64)
    return np.moveaxis((codes * scale).reshape(v.shape), -1, axis)


WIDE = False


def mx_kscale(k):
    if not WIDE:
        return np.ones(k)
    levels = np.array([10, -10, 5, -5, 0])
    if k % 512:
        return np.exp2(np.random.permutation(np.resize(levels, k // 32))).repeat(32)
    a = np.empty((k // 512, 16))
    for p in range(k // 512):
        a[p, :8] = np.random.permutation(np.resize(levels, 8))
        for g in range(8):
            far = levels[np.abs(levels - a[p, g]) >= 10]
            a[p, g + 8] = far[np.random.randint(len(far))]
    return np.exp2(a.ravel()).repeat(32)


def f64(x):
    return np.asarray(x).astype(np.float64)


def striped8(idx):
    return np.asarray(idx).reshape(8, -1, 16).transpose(0, 2, 1).reshape(128, -1).astype(np.uint16)


def unstriped8(offs):
    return offs.reshape(8, 16, -1).transpose(0, 2, 1).reshape(8, -1).astype(np.int64)


def pick8(x, idx, run):
    r = np.arange(len(x))
    return x[r[:, None], idx[r % (8 * run) // run]]


E2M1 = np.array([0.0, 0.5, 1.0, 1.5, 2.0, 3.0, 4.0, 6.0, -0.0, -0.5, -1.0, -1.5, -2.0, -3.0, -4.0, -6.0])


def pack_weight(w, fmt):
    k, n = w.shape
    w = f64(np.asarray(w, np.float32).astype(ml_dtypes.bfloat16)).reshape(k // 32, 32, n)
    amax = np.abs(w).max(1)
    if fmt == "e4m3":
        byte = np.frexp(amax)[1] - 1 + 127 - 7
    else:
        mant, ex = np.frexp(amax / 6.0)
        byte = np.where(mant > 0.5, ex, ex - 1) + 127
    byte = np.clip(np.where(amax > 0, byte, 1), 1, 254)
    scaled = (w * np.exp2(127.0 - byte)[:, None, :]).reshape(k, n).astype(np.float32)
    by_word = np.ascontiguousarray(scaled.reshape(k // 512, 128, 4, n).transpose(0, 1, 3, 2))
    if fmt == "e4m3":
        words = by_word.astype(ml_dtypes.float8_e4m3fn).view(np.uint8)
    else:
        c = by_word.astype(ml_dtypes.float4_e2m1fn).view(np.uint8) & 0xF
        words = (c[..., 0::2] | (c[..., 1::2] << 4)).reshape(k // 512, 128, 2 * n)
    return np.ascontiguousarray(words), np.ascontiguousarray(byte.astype(np.uint8).reshape(k // 512, 16, n))


def unpack_weight(words, scales, fmt):
    g, _, n = scales.shape
    words = np.ascontiguousarray(words).reshape(g, 128, n, -1)
    if fmt == "e4m3":
        vals = words.view(ml_dtypes.float8_e4m3fn).astype(np.float64)
    else:
        nib = np.empty((g, 128, n, 4), np.uint8)
        nib[..., 0::2] = words & 0xF
        nib[..., 1::2] = words >> 4
        vals = E2M1[nib]
    vals = vals * np.repeat(np.exp2(scales.astype(np.float64) - 127.0), 8, axis=1)[..., None]
    return vals.transpose(0, 1, 3, 2).reshape(g * 512, n)


def sigmoid(v):
    return 1.0 / (1.0 + np.exp(-v))


D, K, T, I, Q = 512, 512, 1024, 512, 128


def setup_inputs():
    n = np.random.standard_normal
    idx = np.stack([np.random.permutation(T)[:I] for _ in range(8)])
    idx2 = np.stack([np.random.permutation(T)[:I] for _ in range(8)])
    idx3 = np.stack([np.random.permutation(T)[:I] for _ in range(8)])
    idx4 = np.stack([np.random.permutation(T)[:I] for _ in range(8)])
    fd = mx_kscale(D)
    fk = mx_kscale(K)
    wqp = pack_weight(n((D, K)) * 1.0 / np.sqrt(D) * fd[:, None] * fk, "e4m3")
    keysp = pack_weight(n((K, T)) * 1.0 / np.sqrt(K) / fk[:, None], "e2m1")
    tagsp = pack_weight(n((D, T)) * 0.5 / np.sqrt(D) * fd[:, None], "e4m3")
    return {
        "states": (n((D, Q)) * 0.95 / fd[:, None]).astype(np.float32),
        "wq_words": wqp[0],
        "wq_scales": wqp[1],
        "keys_words": keysp[0],
        "keys_scales": keysp[1],
        "tags_words": tagsp[0],
        "tags_scales": tagsp[1],
        "thr": (np.random.uniform(-0.6, 0.6, (Q, 1))).astype(np.float32),
        "slope": (np.random.uniform(0.8, 2.0, (Q, 1))).astype(np.float32),
        "offs": striped8(idx),
        "offs2": striped8(idx2),
        "offs3": striped8(idx3),
        "offs4": striped8(idx4),
    }


def reference(states, wq_words, wq_scales, keys_words, keys_scales, tags_words, tags_scales, thr, slope, offs, offs2, offs3, offs4):
    idx = unstriped8(offs)
    idx2 = unstriped8(offs2)
    idx3 = unstriped8(offs3)
    idx4 = unstriped8(offs4)
    wqu = unpack_weight(wq_words, wq_scales, "e4m3")
    keysu = unpack_weight(keys_words, keys_scales, "e2m1")
    tagsu = unpack_weight(tags_words, tags_scales, "e4m3")
    statesq = mxq(f64(states), 0, "e4m3")
    qv = wqu.T @ statesq
    qvq = mxq(qv, 0, "e4m3")
    a = qvq.T @ keysu + statesq.T @ tagsu
    ta = np.max(a, axis=1, keepdims=True)
    e1 = np.exp(pick8(a, idx, 16) - ta)
    f1 = np.zeros((Q, T))
    f1[np.arange(Q)[:, None], idx2[np.arange(Q) % 128 // 16]] = e1
    cc = a + f1 * 4.0
    s1 = sigmoid(pick8(cc, idx3, 16) * f64(slope) + f64(thr))
    f2 = np.zeros((Q, T))
    f2[np.arange(Q)[:, None], idx2[np.arange(Q) % 128 // 16]] = s1
    dd = cc + f2
    y = pick8(dd, idx4, 16)
    return y

@@ -1,0 +1,136 @@
+from contextlib import ExitStack
+
+import concourse.mybir as mybir
+
+D, K, T, SLOTS, Q = 512, 512, 1024, 512, 128
+FLOPS = 2 * D * K * Q + 2 * K * Q * T + 2 * D * Q * T
+
+F32 = mybir.dt.float32
+BF16 = mybir.dt.bfloat16
+I32 = mybir.dt.int32
+U32 = mybir.dt.uint32
+U16 = mybir.dt.uint16
+U8 = mybir.dt.uint8
+FP8X4 = mybir.dt.float8_e4m3fn_x4
+FP4X4 = mybir.dt.float4_e2m1fn_x4
+ALU = mybir.AluOpType
+ACT = mybir.ActivationFunctionType
+AXIS = mybir.AxisListType
+
+P = 128
+PACK = 4
+HALF = SLOTS // 2
+LIST_COLS = SLOTS // 16
+PIECES = (256, 256, 512)
+
+
+def tile_attend_echoed_madeparts_kernel(tc, states, wq_words, wq_scales, keys_words, keys_scales,
+                                         tags_words, tags_scales, thr, slope, offs, offs2, offs3, offs4, out):
+    nc = tc.nc
+    with ExitStack() as ctx:
+        sb = ctx.enter_context(tc.tile_pool(name="sb", bufs=1))
+        ps = ctx.enter_context(tc.psum_pool(name="ps", bufs=1))
+
+        def scale_rows(queue, plane, rows, quadrant):
+            queue.dma_start(out=plane[32 * quadrant : 32 * quadrant + 4, :].bitcast(I32),
+                            in_=rows[0, 4 * quadrant : 4 * quadrant + 4, :].bitcast(I32))
+
+        wq_plane_raw = sb.tile([P, K], U8, name="wq_plane_raw", align_bytes=64)
+        tags_plane = sb.tile([P, T], U8, name="tags_plane", align_bytes=64)
+        keys_plane = sb.tile([P, T], U8, name="keys_plane", align_bytes=64)
+        placed = sb.tile([P, T], F32, name="placed", align_bytes=64)
+        nc.vector.memset(wq_plane_raw[:].bitcast(U32), 0)
+        nc.vector.memset(tags_plane[:].bitcast(U32), 0)
+        nc.gpsimd.memset(keys_plane[:].bitcast(U32), 0)
+        nc.vector.memset(placed[:], 0.0)
+
+        states_raw = sb.tile([P, PACK, Q], F32, name="states_raw", align_bytes=64)
+        wq_raw = sb.tile([P, K], U32, name="wq_raw", align_bytes=64)
+        tags_codes = sb.tile([P, T], U32, name="tags_codes", align_bytes=64)
+        keys_codes = sb.tile([P, 2 * T], U8, name="keys_codes", align_bytes=64)
+        nc.sync.dma_start(out=states_raw[:], in_=states.rearrange("(p j) q -> p j q", j=PACK))
+        nc.sync.dma_start(out=wq_raw[:].bitcast(I32), in_=wq_words[0].rearrange("p n j -> p (n j)").bitcast(I32))
+        for quadrant in range(4):
+            scale_rows(nc.scalar, wq_plane_raw, wq_scales, quadrant)
+        nc.sync.dma_start(out=tags_codes[:].bitcast(I32), in_=tags_words[0].rearrange("p n j -> p (n j)").bitcast(I32))
+        scale_rows(nc.scalar, tags_plane, tags_scales, 0)
+        nc.sync.dma_start(out=keys_codes[:].bitcast(I32), in_=keys_words[0].bitcast(I32))
+        scale_rows(nc.sync, keys_plane, keys_scales, 0)
+        for quadrant in range(1, 4):
+            scale_rows(nc.scalar, tags_plane, tags_scales, quadrant)
+        scale_rows(nc.scalar, keys_plane, keys_scales, 1)
+        for quadrant in range(2, 4):
+            scale_rows(nc.gpsimd, keys_plane, keys_scales, quadrant)
+        lists = []
+        for n, source in enumerate((offs, offs2, offs3, offs4)):
+            held = sb.tile([P, LIST_COLS], U16, name="list%d" % n)
+            nc.sync.dma_start(held[:], source)
+            lists.append(held)
+        exp_list, place_list, gate_list, out_list = lists
+        thr_col = sb.tile([P, 1], F32, name="thr_col")
+        slope_col = sb.tile([P, 1], F32, name="slope_col")
+        nc.sync.dma_start(out=thr_col[:], in_=thr)
+        nc.sync.dma_start(out=slope_col[:], in_=slope)
+
+        wq_plane = sb.tile([P, K], U8, name="wq_plane", align_bytes=64)
+        nc.vector.tensor_copy(out=wq_plane[:].rearrange("p (j m) -> p m j", j=PACK),
+                              in_=wq_plane_raw[:].rearrange("p (m j) -> p m j", j=PACK))
+
+        states_bf = sb.tile([P, Q * PACK], BF16, name="states_bf", align_bytes=64)
+        nc.vector.tensor_copy(out=states_bf[:].rearrange("p (c i j) -> p c j i", i=4, j=PACK),
+                              in_=states_raw[:].rearrange("p j (c i) -> p c j i", i=4))
+        wq_codes = sb.tile([P, K], U32, name="wq_codes", align_bytes=64)
+        nc.vector.tensor_copy(out=wq_codes[:].rearrange("p (j m) -> p m j", j=PACK),
+                              in_=wq_raw[:].rearrange("p (m j) -> p m j", j=PACK))
+        states_codes = sb.tile([P, Q], U32, name="states_codes", align_bytes=64)
+        states_plane = sb.tile([P, Q], U8, name="states_plane", align_bytes=64)
+        nc.vector.quantize_mx(out=states_codes[:].bitcast(FP8X4), scales=states_plane[:], in_=states_bf[:])
+
+        qv_bank = ps.tile([P, PACK, Q], F32, name="qv_bank")
+        for j in range(PACK):
+            cols = slice(j * P, (j + 1) * P)
+            nc.tensor.matmul_mx(out=qv_bank[:, j, :], lhsT=wq_codes[:, cols].bitcast(FP8X4), lhsT_scale=wq_plane[:, cols],
+                                rhs=states_codes[:].bitcast(FP8X4), rhs_scale=states_plane[:], start=True, stop=True)
+        qv_bf = sb.tile([P, Q * PACK], BF16, name="qv_bf", align_bytes=64)
+        nc.vector.tensor_copy(out=qv_bf[:].rearrange("p (q j) -> p q j", j=PACK), in_=qv_bank[:].rearrange("p j q -> p q j"))
+        qv_codes = sb.tile([P, Q], U32, name="qv_codes", align_bytes=64)
+        qv_plane = sb.tile([P, Q], U8, name="qv_plane", align_bytes=64)
+        nc.vector.quantize_mx(out=qv_codes[:].bitcast(FP8X4), scales=qv_plane[:], in_=qv_bf[:])
+
+        spans = [slice(sum(PIECES[:n]), sum(PIECES[: n + 1])) for n in range(len(PIECES))]
+        banks = [ps.tile([P, width], F32, name="score_bank%d" % n) for n, width in enumerate(PIECES)]
+        for bank, span in zip(banks, spans):
+            nc.tensor.matmul_mx(out=bank[:], lhsT=states_codes[:].bitcast(FP8X4), lhsT_scale=states_plane[:],
+                                rhs=tags_codes[:, span].bitcast(FP8X4), rhs_scale=tags_plane[:, span], start=True, stop=False)
+        score = sb.tile([P, T], F32, name="score", align_bytes=64)
+        piece_max = sb.tile([P, len(PIECES)], F32, name="piece_max")
+        for n, (bank, span) in enumerate(zip(banks, spans)):
+            nc.tensor.matmul_mx(out=bank[:], lhsT=qv_codes[:].bitcast(FP8X4), lhsT_scale=qv_plane[:],
+                                rhs=keys_codes[:, 2 * span.start : 2 * span.stop].bitcast(FP4X4), rhs_scale=keys_plane[:, span],
+                                start=False, stop=True)
+            nc.vector.tensor_scalar(out=score[:, span], in0=bank[:], scalar1=1.0, scalar2=None, op0=ALU.mult, op1=ALU.max,
+                                    accum_out=piece_max[:, n : n + 1])
+        minus_top = sb.tile([P, 1], F32, name="minus_top")
+        nc.vector.tensor_reduce(out=minus_top[:], in_=piece_max[:], axis=AXIS.X, op=ALU.max, negate=True)
+
+        halves = [(slice(h * HALF, (h + 1) * HALF), slice(h * HALF // 16, (h + 1) * HALF // 16)) for h in range(2)]
+        e1 = [sb.tile([P, HALF], F32, name="e1_%d" % h) for h in range(2)]
+        for h, (slots, entries) in enumerate(halves):
+            nc.scalar.activation(out=e1[h][:], in_=score[:].indirect(exp_list[:, entries]), func=ACT.Exp, bias=minus_top[:])
+            nc.vector.tensor_copy(out=placed[:].indirect(place_list[:, entries]), in_=e1[h][:])
+        cc = sb.tile([P, T], F32, name="cc", align_bytes=64)
+        nc.vector.scalar_tensor_tensor(out=cc[:], in0=placed[:], scalar=4.0, in1=score[:], op0=ALU.mult, op1=ALU.add)
+
+        s1 = [sb.tile([P, HALF], F32, name="s1_%d" % h) for h in range(2)]
+        for h, (slots, entries) in enumerate(halves):
+            nc.scalar.activation(out=s1[h][:], in_=cc[:].indirect(gate_list[:, entries]), func=ACT.Sigmoid,
+                                 bias=thr_col[:], scale=slope_col[:])
+            nc.vector.tensor_copy(out=placed[:].indirect(place_list[:, entries]), in_=s1[h][:])
+        dd = sb.tile([P, T], F32, name="dd", align_bytes=64)
+        nc.vector.tensor_tensor(out=dd[:], in0=placed[:], in1=cc[:], op=ALU.add)
+
+        result = [sb.tile([P, HALF], F32, name="result%d" % h) for h in range(2)]
+        nc.vector.tensor_copy(out=result[0][:], in_=dd[:].indirect(out_list[:, halves[0][1]]))
+        nc.sync.dma_start(out=out[:, halves[0][0]], in_=result[0][:])
+        nc.scalar.activation(out=result[1][:], in_=dd[:].indirect(out_list[:, halves[1][1]]), func=ACT.Copy)
+        nc.scalar.dma_start(out=out[:, halves[1][0]], in_=result[1][:])

@@ -22,6 +22,7 @@ PACK = 4
 HALF = SLOTS // 2
 LIST_COLS = SLOTS // 16
 PIECES = (256, 256, 512)
+CAST_SPLIT = 22
 
 
 def tile_attend_echoed_madeparts_kernel(tc, states, wq_words, wq_scales, keys_words, keys_scales,
@@ -39,28 +40,26 @@ def tile_attend_echoed_madeparts_kernel(tc, states, wq_words, wq_scales, keys_wo
         tags_plane = sb.tile([P, T], U8, name="tags_plane", align_bytes=64)
         keys_plane = sb.tile([P, T], U8, name="keys_plane", align_bytes=64)
         placed = sb.tile([P, T], F32, name="placed", align_bytes=64)
-        nc.vector.memset(wq_plane_raw[:].bitcast(U32), 0)
-        nc.vector.memset(tags_plane[:].bitcast(U32), 0)
-        nc.gpsimd.memset(keys_plane[:].bitcast(U32), 0)
+        fours = sb.tile([P, HALF], F32, name="fours", align_bytes=64)
+        for plane in (wq_plane_raw, tags_plane, keys_plane):
+            nc.gpsimd.memset(plane[:].bitcast(U32), 0)
         nc.vector.memset(placed[:], 0.0)
+        nc.vector.memset(fours[:], 4.0)
 
         states_raw = sb.tile([P, PACK, Q], F32, name="states_raw", align_bytes=64)
         wq_raw = sb.tile([P, K], U32, name="wq_raw", align_bytes=64)
         tags_codes = sb.tile([P, T], U32, name="tags_codes", align_bytes=64)
         keys_codes = sb.tile([P, 2 * T], U8, name="keys_codes", align_bytes=64)
         nc.sync.dma_start(out=states_raw[:], in_=states.rearrange("(p j) q -> p j q", j=PACK))
-        nc.sync.dma_start(out=wq_raw[:].bitcast(I32), in_=wq_words[0].rearrange("p n j -> p (n j)").bitcast(I32))
         for quadrant in range(4):
-            scale_rows(nc.scalar, wq_plane_raw, wq_scales, quadrant)
+            scale_rows(nc.scalar if quadrant < 2 else nc.sync, wq_plane_raw, wq_scales, quadrant)
+        nc.sync.dma_start(out=wq_raw[:].bitcast(I32), in_=wq_words[0].rearrange("p n j -> p (n j)").bitcast(I32))
         nc.sync.dma_start(out=tags_codes[:].bitcast(I32), in_=tags_words[0].rearrange("p n j -> p (n j)").bitcast(I32))
-        scale_rows(nc.scalar, tags_plane, tags_scales, 0)
+        for quadrant in range(4):
+            scale_rows(nc.sync, tags_plane, tags_scales, quadrant)
         nc.sync.dma_start(out=keys_codes[:].bitcast(I32), in_=keys_words[0].bitcast(I32))
-        scale_rows(nc.sync, keys_plane, keys_scales, 0)
-        for quadrant in range(1, 4):
-            scale_rows(nc.scalar, tags_plane, tags_scales, quadrant)
-        scale_rows(nc.scalar, keys_plane, keys_scales, 1)
-        for quadrant in range(2, 4):
-            scale_rows(nc.gpsimd, keys_plane, keys_scales, quadrant)
+        for quadrant in range(4):
+            scale_rows(nc.sync, keys_plane, keys_scales, quadrant)
         lists = []
         for n, source in enumerate((offs, offs2, offs3, offs4)):
             held = sb.tile([P, LIST_COLS], U16, name="list%d" % n)
@@ -72,16 +71,17 @@ def tile_attend_echoed_madeparts_kernel(tc, states, wq_words, wq_scales, keys_wo
         nc.sync.dma_start(out=thr_col[:], in_=thr)
         nc.sync.dma_start(out=slope_col[:], in_=slope)
 
+        states_bf = sb.tile([P, Q * PACK], BF16, name="states_bf", align_bytes=64)
+        woven = states_bf[:].rearrange("p (c i j) -> p c j i", i=4, j=PACK)
+        rows = states_raw[:].rearrange("p j (c i) -> p c j i", i=4)
+        nc.vector.tensor_copy(out=woven[:, :CAST_SPLIT], in_=rows[:, :CAST_SPLIT])
+        nc.scalar.activation(out=woven[:, CAST_SPLIT:], in_=rows[:, CAST_SPLIT:], func=ACT.Copy)
         wq_plane = sb.tile([P, K], U8, name="wq_plane", align_bytes=64)
         nc.vector.tensor_copy(out=wq_plane[:].rearrange("p (j m) -> p m j", j=PACK),
                               in_=wq_plane_raw[:].rearrange("p (m j) -> p m j", j=PACK))
-
-        states_bf = sb.tile([P, Q * PACK], BF16, name="states_bf", align_bytes=64)
-        nc.vector.tensor_copy(out=states_bf[:].rearrange("p (c i j) -> p c j i", i=4, j=PACK),
-                              in_=states_raw[:].rearrange("p j (c i) -> p c j i", i=4))
         wq_codes = sb.tile([P, K], U32, name="wq_codes", align_bytes=64)
-        nc.vector.tensor_copy(out=wq_codes[:].rearrange("p (j m) -> p m j", j=PACK),
-                              in_=wq_raw[:].rearrange("p (m j) -> p m j", j=PACK))
+        nc.scalar.copy(out=wq_codes[:].rearrange("p (j m) -> p m j", j=PACK),
+                       in_=wq_raw[:].rearrange("p (m j) -> p m j", j=PACK))
         states_codes = sb.tile([P, Q], U32, name="states_codes", align_bytes=64)
         states_plane = sb.tile([P, Q], U8, name="states_plane", align_bytes=64)
         nc.vector.quantize_mx(out=states_codes[:].bitcast(FP8X4), scales=states_plane[:], in_=states_bf[:])
@@ -92,7 +92,7 @@ def tile_attend_echoed_madeparts_kernel(tc, states, wq_words, wq_scales, keys_wo
             nc.tensor.matmul_mx(out=qv_bank[:, j, :], lhsT=wq_codes[:, cols].bitcast(FP8X4), lhsT_scale=wq_plane[:, cols],
                                 rhs=states_codes[:].bitcast(FP8X4), rhs_scale=states_plane[:], start=True, stop=True)
         qv_bf = sb.tile([P, Q * PACK], BF16, name="qv_bf", align_bytes=64)
-        nc.vector.tensor_copy(out=qv_bf[:].rearrange("p (q j) -> p q j", j=PACK), in_=qv_bank[:].rearrange("p j q -> p q j"))
+        nc.scalar.copy(out=qv_bf[:].rearrange("p (q j) -> p q j", j=PACK), in_=qv_bank[:].rearrange("p j q -> p q j"))
         qv_codes = sb.tile([P, Q], U32, name="qv_codes", align_bytes=64)
         qv_plane = sb.tile([P, Q], U8, name="qv_plane", align_bytes=64)
         nc.vector.quantize_mx(out=qv_codes[:].bitcast(FP8X4), scales=qv_plane[:], in_=qv_bf[:])
@@ -113,21 +113,29 @@ def tile_attend_echoed_madeparts_kernel(tc, states, wq_words, wq_scales, keys_wo
         minus_top = sb.tile([P, 1], F32, name="minus_top")
         nc.vector.tensor_reduce(out=minus_top[:], in_=piece_max[:], axis=AXIS.X, op=ALU.max, negate=True)
 
+        def add_scores(total):
+            nc.gpsimd.tensor_tensor(out=total[:, spans[0]], in0=placed[:, spans[0]], in1=score[:, spans[0]], op=ALU.add)
+            for bank, span in zip(banks[1:], spans[1:]):
+                nc.vector.tensor_tensor(out=total[:, span], in0=placed[:, span], in1=bank[:], op=ALU.add)
+
         halves = [(slice(h * HALF, (h + 1) * HALF), slice(h * HALF // 16, (h + 1) * HALF // 16)) for h in range(2)]
         e1 = [sb.tile([P, HALF], F32, name="e1_%d" % h) for h in range(2)]
         for h, (slots, entries) in enumerate(halves):
             nc.scalar.activation(out=e1[h][:], in_=score[:].indirect(exp_list[:, entries]), func=ACT.Exp, bias=minus_top[:])
-            nc.vector.tensor_copy(out=placed[:].indirect(place_list[:, entries]), in_=e1[h][:])
+            nc.vector.tensor_tensor(out=placed[:].indirect(place_list[:, entries]), in0=e1[h][:], in1=fours[:], op=ALU.mult)
         cc = sb.tile([P, T], F32, name="cc", align_bytes=64)
-        nc.vector.scalar_tensor_tensor(out=cc[:], in0=placed[:], scalar=4.0, in1=score[:], op0=ALU.mult, op1=ALU.add)
+        add_scores(cc)
+        e4 = [sb.tile([P, HALF], F32, name="e4_%d" % h) for h in range(2)]
+        for h in range(2):
+            nc.scalar.activation(out=e4[h][:], in_=e1[h][:], func=ACT.Copy, scale=4.0)
 
         s1 = [sb.tile([P, HALF], F32, name="s1_%d" % h) for h in range(2)]
         for h, (slots, entries) in enumerate(halves):
             nc.scalar.activation(out=s1[h][:], in_=cc[:].indirect(gate_list[:, entries]), func=ACT.Sigmoid,
                                  bias=thr_col[:], scale=slope_col[:])
-            nc.vector.tensor_copy(out=placed[:].indirect(place_list[:, entries]), in_=s1[h][:])
+            nc.vector.tensor_tensor(out=placed[:].indirect(place_list[:, entries]), in0=s1[h][:], in1=e4[h][:], op=ALU.add)
         dd = sb.tile([P, T], F32, name="dd", align_bytes=64)
-        nc.vector.tensor_tensor(out=dd[:], in0=placed[:], in1=cc[:], op=ALU.add)
+        add_scores(dd)
 
         result = [sb.tile([P, HALF], F32, name="result%d" % h) for h in range(2)]
         nc.vector.tensor_copy(out=result[0][:], in_=dd[:].indirect(out_list[:, halves[0][1]]))

@@ -21,7 +21,7 @@ P = 128
 PACK = 4
 HALF = SLOTS // 2
 LIST_COLS = SLOTS // 16
-PIECES = (256, 256, 512)
+PIECES = (128, 256, 256, 256, 128)
 CAST_SPLIT = 22
 
 
@@ -40,11 +40,10 @@ def tile_attend_echoed_madeparts_kernel(tc, states, wq_words, wq_scales, keys_wo
         tags_plane = sb.tile([P, T], U8, name="tags_plane", align_bytes=64)
         keys_plane = sb.tile([P, T], U8, name="keys_plane", align_bytes=64)
         placed = sb.tile([P, T], F32, name="placed", align_bytes=64)
-        fours = sb.tile([P, HALF], F32, name="fours", align_bytes=64)
-        for plane in (wq_plane_raw, tags_plane, keys_plane):
-            nc.gpsimd.memset(plane[:].bitcast(U32), 0)
+        nc.gpsimd.memset(wq_plane_raw[:].bitcast(U32), 0)
+        for plane in (tags_plane, keys_plane):
+            nc.vector.memset(plane[:].bitcast(U32), 0)
         nc.vector.memset(placed[:], 0.0)
-        nc.vector.memset(fours[:], 4.0)
 
         states_raw = sb.tile([P, PACK, Q], F32, name="states_raw", align_bytes=64)
         wq_raw = sb.tile([P, K], U32, name="wq_raw", align_bytes=64)
@@ -56,10 +55,10 @@ def tile_attend_echoed_madeparts_kernel(tc, states, wq_words, wq_scales, keys_wo
         nc.sync.dma_start(out=wq_raw[:].bitcast(I32), in_=wq_words[0].rearrange("p n j -> p (n j)").bitcast(I32))
         nc.sync.dma_start(out=tags_codes[:].bitcast(I32), in_=tags_words[0].rearrange("p n j -> p (n j)").bitcast(I32))
         for quadrant in range(4):
-            scale_rows(nc.sync, tags_plane, tags_scales, quadrant)
+            scale_rows(nc.sync if quadrant < 3 else nc.gpsimd, tags_plane, tags_scales, quadrant)
         nc.sync.dma_start(out=keys_codes[:].bitcast(I32), in_=keys_words[0].bitcast(I32))
         for quadrant in range(4):
-            scale_rows(nc.sync, keys_plane, keys_scales, quadrant)
+            scale_rows(nc.sync if quadrant < 3 else nc.gpsimd, keys_plane, keys_scales, quadrant)
         lists = []
         for n, source in enumerate((offs, offs2, offs3, offs4)):
             held = sb.tile([P, LIST_COLS], U16, name="list%d" % n)
@@ -80,31 +79,34 @@ def tile_attend_echoed_madeparts_kernel(tc, states, wq_words, wq_scales, keys_wo
         nc.vector.tensor_copy(out=wq_plane[:].rearrange("p (j m) -> p m j", j=PACK),
                               in_=wq_plane_raw[:].rearrange("p (m j) -> p m j", j=PACK))
         wq_codes = sb.tile([P, K], U32, name="wq_codes", align_bytes=64)
-        nc.scalar.copy(out=wq_codes[:].rearrange("p (j m) -> p m j", j=PACK),
-                       in_=wq_raw[:].rearrange("p (m j) -> p m j", j=PACK))
         states_codes = sb.tile([P, Q], U32, name="states_codes", align_bytes=64)
         states_plane = sb.tile([P, Q], U8, name="states_plane", align_bytes=64)
         nc.vector.quantize_mx(out=states_codes[:].bitcast(FP8X4), scales=states_plane[:], in_=states_bf[:])
 
-        qv_bank = ps.tile([P, PACK, Q], F32, name="qv_bank")
+        dealt = wq_codes[:].rearrange("p (j m) -> p m j", j=PACK)
+        arrived = wq_raw[:].rearrange("p (m j) -> p m j", j=PACK)
+        nc.vector.tensor_copy(out=dealt[:, :, :2], in_=arrived[:, :, :2])
+        nc.scalar.copy(out=dealt[:, :, 2:], in_=arrived[:, :, 2:])
+        qv_banks = [ps.tile([P, 2, Q], F32, name="qv_bank%d" % u) for u in range(2)]
         for j in range(PACK):
             cols = slice(j * P, (j + 1) * P)
-            nc.tensor.matmul_mx(out=qv_bank[:, j, :], lhsT=wq_codes[:, cols].bitcast(FP8X4), lhsT_scale=wq_plane[:, cols],
+            nc.tensor.matmul_mx(out=qv_banks[j // 2][:, j % 2, :], lhsT=wq_codes[:, cols].bitcast(FP8X4), lhsT_scale=wq_plane[:, cols],
                                 rhs=states_codes[:].bitcast(FP8X4), rhs_scale=states_plane[:], start=True, stop=True)
         qv_bf = sb.tile([P, Q * PACK], BF16, name="qv_bf", align_bytes=64)
-        nc.scalar.copy(out=qv_bf[:].rearrange("p (q j) -> p q j", j=PACK), in_=qv_bank[:].rearrange("p j q -> p q j"))
+        qv_woven = qv_bf[:].rearrange("p (q j) -> p q j", j=PACK)
+        nc.vector.tensor_copy(out=qv_woven[:, :, :2], in_=qv_banks[0][:].rearrange("p j q -> p q j"))
+        nc.scalar.copy(out=qv_woven[:, :, 2:], in_=qv_banks[1][:].rearrange("p j q -> p q j"))
         qv_codes = sb.tile([P, Q], U32, name="qv_codes", align_bytes=64)
         qv_plane = sb.tile([P, Q], U8, name="qv_plane", align_bytes=64)
         nc.vector.quantize_mx(out=qv_codes[:].bitcast(FP8X4), scales=qv_plane[:], in_=qv_bf[:])
 
         spans = [slice(sum(PIECES[:n]), sum(PIECES[: n + 1])) for n in range(len(PIECES))]
         banks = [ps.tile([P, width], F32, name="score_bank%d" % n) for n, width in enumerate(PIECES)]
-        for bank, span in zip(banks, spans):
-            nc.tensor.matmul_mx(out=bank[:], lhsT=states_codes[:].bitcast(FP8X4), lhsT_scale=states_plane[:],
-                                rhs=tags_codes[:, span].bitcast(FP8X4), rhs_scale=tags_plane[:, span], start=True, stop=False)
         score = sb.tile([P, T], F32, name="score", align_bytes=64)
         piece_max = sb.tile([P, len(PIECES)], F32, name="piece_max")
         for n, (bank, span) in enumerate(zip(banks, spans)):
+            nc.tensor.matmul_mx(out=bank[:], lhsT=states_codes[:].bitcast(FP8X4), lhsT_scale=states_plane[:],
+                                rhs=tags_codes[:, span].bitcast(FP8X4), rhs_scale=tags_plane[:, span], start=True, stop=False)
             nc.tensor.matmul_mx(out=bank[:], lhsT=qv_codes[:].bitcast(FP8X4), lhsT_scale=qv_plane[:],
                                 rhs=keys_codes[:, 2 * span.start : 2 * span.stop].bitcast(FP4X4), rhs_scale=keys_plane[:, span],
                                 start=False, stop=True)
@@ -113,29 +115,21 @@ def tile_attend_echoed_madeparts_kernel(tc, states, wq_words, wq_scales, keys_wo
         minus_top = sb.tile([P, 1], F32, name="minus_top")
         nc.vector.tensor_reduce(out=minus_top[:], in_=piece_max[:], axis=AXIS.X, op=ALU.max, negate=True)
 
-        def add_scores(total):
-            nc.gpsimd.tensor_tensor(out=total[:, spans[0]], in0=placed[:, spans[0]], in1=score[:, spans[0]], op=ALU.add)
-            for bank, span in zip(banks[1:], spans[1:]):
-                nc.vector.tensor_tensor(out=total[:, span], in0=placed[:, span], in1=bank[:], op=ALU.add)
-
         halves = [(slice(h * HALF, (h + 1) * HALF), slice(h * HALF // 16, (h + 1) * HALF // 16)) for h in range(2)]
         e1 = [sb.tile([P, HALF], F32, name="e1_%d" % h) for h in range(2)]
         for h, (slots, entries) in enumerate(halves):
             nc.scalar.activation(out=e1[h][:], in_=score[:].indirect(exp_list[:, entries]), func=ACT.Exp, bias=minus_top[:])
-            nc.vector.tensor_tensor(out=placed[:].indirect(place_list[:, entries]), in0=e1[h][:], in1=fours[:], op=ALU.mult)
+            nc.vector.tensor_copy(out=placed[:].indirect(place_list[:, entries]), in_=e1[h][:])
         cc = sb.tile([P, T], F32, name="cc", align_bytes=64)
-        add_scores(cc)
-        e4 = [sb.tile([P, HALF], F32, name="e4_%d" % h) for h in range(2)]
-        for h in range(2):
-            nc.scalar.activation(out=e4[h][:], in_=e1[h][:], func=ACT.Copy, scale=4.0)
+        nc.vector.scalar_tensor_tensor(out=cc[:], in0=placed[:], scalar=4.0, in1=score[:], op0=ALU.mult, op1=ALU.add)
 
         s1 = [sb.tile([P, HALF], F32, name="s1_%d" % h) for h in range(2)]
         for h, (slots, entries) in enumerate(halves):
             nc.scalar.activation(out=s1[h][:], in_=cc[:].indirect(gate_list[:, entries]), func=ACT.Sigmoid,
                                  bias=thr_col[:], scale=slope_col[:])
-            nc.vector.tensor_tensor(out=placed[:].indirect(place_list[:, entries]), in0=s1[h][:], in1=e4[h][:], op=ALU.add)
+            nc.vector.tensor_copy(out=placed[:].indirect(place_list[:, entries]), in_=s1[h][:])
         dd = sb.tile([P, T], F32, name="dd", align_bytes=64)
-        add_scores(dd)
+        nc.vector.tensor_tensor(out=dd[:], in0=placed[:], in1=cc[:], op=ALU.add)
 
         result = [sb.tile([P, HALF], F32, name="result%d" % h) for h in range(2)]
         nc.vector.tensor_copy(out=result[0][:], in_=dd[:].indirect(out_list[:, halves[0][1]]))

from contextlib import ExitStack

import concourse.mybir as mybir

D, K, T, SLOTS, Q = 512, 512, 1024, 512, 128
FLOPS = 2 * D * K * Q + 2 * K * Q * T + 2 * D * Q * T

F32 = mybir.dt.float32
BF16 = mybir.dt.bfloat16
I32 = mybir.dt.int32
U32 = mybir.dt.uint32
U16 = mybir.dt.uint16
U8 = mybir.dt.uint8
FP8X4 = mybir.dt.float8_e4m3fn_x4
FP4X4 = mybir.dt.float4_e2m1fn_x4
ALU = mybir.AluOpType
ACT = mybir.ActivationFunctionType
AXIS = mybir.AxisListType

P = 128
PACK = 4
HALF = SLOTS // 2
LIST_COLS = SLOTS // 16
PIECES = (128, 256, 256, 256, 128)
CAST_SPLIT = 22


def tile_attend_echoed_madeparts_kernel(tc, states, wq_words, wq_scales, keys_words, keys_scales,
                                         tags_words, tags_scales, thr, slope, offs, offs2, offs3, offs4, out):
    nc = tc.nc
    with ExitStack() as ctx:
        sb = ctx.enter_context(tc.tile_pool(name="sb", bufs=1))
        ps = ctx.enter_context(tc.psum_pool(name="ps", bufs=1))

        def scale_rows(queue, plane, rows, quadrant):
            queue.dma_start(out=plane[32 * quadrant : 32 * quadrant + 4, :].bitcast(I32),
                            in_=rows[0, 4 * quadrant : 4 * quadrant + 4, :].bitcast(I32))

        wq_plane_raw = sb.tile([P, K], U8, name="wq_plane_raw", align_bytes=64)
        tags_plane = sb.tile([P, T], U8, name="tags_plane", align_bytes=64)
        keys_plane = sb.tile([P, T], U8, name="keys_plane", align_bytes=64)
        placed = sb.tile([P, T], F32, name="placed", align_bytes=64)
        nc.gpsimd.memset(wq_plane_raw[:].bitcast(U32), 0)
        for plane in (tags_plane, keys_plane):
            nc.vector.memset(plane[:].bitcast(U32), 0)
        nc.vector.memset(placed[:], 0.0)

        states_raw = sb.tile([P, PACK, Q], F32, name="states_raw", align_bytes=64)
        wq_raw = sb.tile([P, K], U32, name="wq_raw", align_bytes=64)
        tags_codes = sb.tile([P, T], U32, name="tags_codes", align_bytes=64)
        keys_codes = sb.tile([P, 2 * T], U8, name="keys_codes", align_bytes=64)
        nc.sync.dma_start(out=states_raw[:], in_=states.rearrange("(p j) q -> p j q", j=PACK))
        for quadrant in range(4):
            scale_rows(nc.scalar if quadrant < 2 else nc.sync, wq_plane_raw, wq_scales, quadrant)
        nc.sync.dma_start(out=wq_raw[:].bitcast(I32), in_=wq_words[0].rearrange("p n j -> p (n j)").bitcast(I32))
        nc.sync.dma_start(out=tags_codes[:].bitcast(I32), in_=tags_words[0].rearrange("p n j -> p (n j)").bitcast(I32))
        for quadrant in range(4):
            scale_rows(nc.sync if quadrant < 3 else nc.gpsimd, tags_plane, tags_scales, quadrant)
        nc.sync.dma_start(out=keys_codes[:].bitcast(I32), in_=keys_words[0].bitcast(I32))
        for quadrant in range(4):
            scale_rows(nc.sync if quadrant < 3 else nc.gpsimd, keys_plane, keys_scales, quadrant)
        lists = []
        for n, source in enumerate((offs, offs2, offs3, offs4)):
            held = sb.tile([P, LIST_COLS], U16, name="list%d" % n)
            nc.sync.dma_start(held[:], source)
            lists.append(held)
        exp_list, place_list, gate_list, out_list = lists
        thr_col = sb.tile([P, 1], F32, name="thr_col")
        slope_col = sb.tile([P, 1], F32, name="slope_col")
        nc.sync.dma_start(out=thr_col[:], in_=thr)
        nc.sync.dma_start(out=slope_col[:], in_=slope)

        states_bf = sb.tile([P, Q * PACK], BF16, name="states_bf", align_bytes=64)
        woven = states_bf[:].rearrange("p (c i j) -> p c j i", i=4, j=PACK)
        rows = states_raw[:].rearrange("p j (c i) -> p c j i", i=4)
        nc.vector.tensor_copy(out=woven[:, :CAST_SPLIT], in_=rows[:, :CAST_SPLIT])
        nc.scalar.activation(out=woven[:, CAST_SPLIT:], in_=rows[:, CAST_SPLIT:], func=ACT.Copy)
        wq_plane = sb.tile([P, K], U8, name="wq_plane", align_bytes=64)
        nc.vector.tensor_copy(out=wq_plane[:].rearrange("p (j m) -> p m j", j=PACK),
                              in_=wq_plane_raw[:].rearrange("p (m j) -> p m j", j=PACK))
        wq_codes = sb.tile([P, K], U32, name="wq_codes", align_bytes=64)
        states_codes = sb.tile([P, Q], U32, name="states_codes", align_bytes=64)
        states_plane = sb.tile([P, Q], U8, name="states_plane", align_bytes=64)
        nc.vector.quantize_mx(out=states_codes[:].bitcast(FP8X4), scales=states_plane[:], in_=states_bf[:])

        dealt = wq_codes[:].rearrange("p (j m) -> p m j", j=PACK)
        arrived = wq_raw[:].rearrange("p (m j) -> p m j", j=PACK)
        nc.vector.tensor_copy(out=dealt[:, :, :2], in_=arrived[:, :, :2])
        nc.scalar.copy(out=dealt[:, :, 2:], in_=arrived[:, :, 2:])
        qv_banks = [ps.tile([P, 2, Q], F32, name="qv_bank%d" % u) for u in range(2)]
        for j in range(PACK):
            cols = slice(j * P, (j + 1) * P)
            nc.tensor.matmul_mx(out=qv_banks[j // 2][:, j % 2, :], lhsT=wq_codes[:, cols].bitcast(FP8X4), lhsT_scale=wq_plane[:, cols],
                                rhs=states_codes[:].bitcast(FP8X4), rhs_scale=states_plane[:], start=True, stop=True)
        qv_bf = sb.tile([P, Q * PACK], BF16, name="qv_bf", align_bytes=64)
        qv_woven = qv_bf[:].rearrange("p (q j) -> p q j", j=PACK)
        nc.vector.tensor_copy(out=qv_woven[:, :, :2], in_=qv_banks[0][:].rearrange("p j q -> p q j"))
        nc.scalar.copy(out=qv_woven[:, :, 2:], in_=qv_banks[1][:].rearrange("p j q -> p q j"))
        qv_codes = sb.tile([P, Q], U32, name="qv_codes", align_bytes=64)
        qv_plane = sb.tile([P, Q], U8, name="qv_plane", align_bytes=64)
        nc.vector.quantize_mx(out=qv_codes[:].bitcast(FP8X4), scales=qv_plane[:], in_=qv_bf[:])

        spans = [slice(sum(PIECES[:n]), sum(PIECES[: n + 1])) for n in range(len(PIECES))]
        banks = [ps.tile([P, width], F32, name="score_bank%d" % n) for n, width in enumerate(PIECES)]
        score = sb.tile([P, T], F32, name="score", align_bytes=64)
        piece_max = sb.tile([P, len(PIECES)], F32, name="piece_max")
        for n, (bank, span) in enumerate(zip(banks, spans)):
            nc.tensor.matmul_mx(out=bank[:], lhsT=states_codes[:].bitcast(FP8X4), lhsT_scale=states_plane[:],
                                rhs=tags_codes[:, span].bitcast(FP8X4), rhs_scale=tags_plane[:, span], start=True, stop=False)
            nc.tensor.matmul_mx(out=bank[:], lhsT=qv_codes[:].bitcast(FP8X4), lhsT_scale=qv_plane[:],
                                rhs=keys_codes[:, 2 * span.start : 2 * span.stop].bitcast(FP4X4), rhs_scale=keys_plane[:, span],
                                start=False, stop=True)
            nc.vector.tensor_scalar(out=score[:, span], in0=bank[:], scalar1=1.0, scalar2=None, op0=ALU.mult, op1=ALU.max,
                                    accum_out=piece_max[:, n : n + 1])
        minus_top = sb.tile([P, 1], F32, name="minus_top")
        nc.vector.tensor_reduce(out=minus_top[:], in_=piece_max[:], axis=AXIS.X, op=ALU.max, negate=True)

        halves = [(slice(h * HALF, (h + 1) * HALF), slice(h * HALF // 16, (h + 1) * HALF // 16)) for h in range(2)]
        e1 = [sb.tile([P, HALF], F32, name="e1_%d" % h) for h in range(2)]
        for h, (slots, entries) in enumerate(halves):
            nc.scalar.activation(out=e1[h][:], in_=score[:].indirect(exp_list[:, entries]), func=ACT.Exp, bias=minus_top[:])
            nc.vector.tensor_copy(out=placed[:].indirect(place_list[:, entries]), in_=e1[h][:])
        cc = sb.tile([P, T], F32, name="cc", align_bytes=64)
        nc.vector.scalar_tensor_tensor(out=cc[:], in0=placed[:], scalar=4.0, in1=score[:], op0=ALU.mult, op1=ALU.add)

        s1 = [sb.tile([P, HALF], F32, name="s1_%d" % h) for h in range(2)]
        for h, (slots, entries) in enumerate(halves):
            nc.scalar.activation(out=s1[h][:], in_=cc[:].indirect(gate_list[:, entries]), func=ACT.Sigmoid,
                                 bias=thr_col[:], scale=slope_col[:])
            nc.vector.tensor_copy(out=placed[:].indirect(place_list[:, entries]), in_=s1[h][:])
        dd = sb.tile([P, T], F32, name="dd", align_bytes=64)
        nc.vector.tensor_tensor(out=dd[:], in0=placed[:], in1=cc[:], op=ALU.add)

        result = [sb.tile([P, HALF], F32, name="result%d" % h) for h in range(2)]
        nc.vector.tensor_copy(out=result[0][:], in_=dd[:].indirect(out_list[:, halves[0][1]]))
        nc.sync.dma_start(out=out[:, halves[0][0]], in_=result[0][:])
        nc.scalar.activation(out=result[1][:], in_=dd[:].indirect(out_list[:, halves[1][1]]), func=ACT.Copy)
        nc.scalar.dma_start(out=out[:, halves[1][0]], in_=result[1][:])
